import numpy as np
import ml_dtypes


def mxq(x, axis, fmt="e4m3"):
    dtype, down = {"e4m3": (ml_dtypes.float8_e4m3fn, 7), "e5m2": (ml_dtypes.float8_e5m2, 14)}[fmt]
    v = np.moveaxis(np.asarray(x, np.float32).astype(ml_dtypes.bfloat16).astype(np.float64), axis, -1)
    blocks = v.reshape(v.shape[:-1] + (-1, 32))
    amax = np.abs(blocks).max(-1, keepdims=True)
    byte = np.maximum(np.where(amax > 0, np.frexp(amax)[1] - 1 + 127, 0) - down, 1)
    scale = np.exp2(byte - 127.0)
    codes = (blocks / scale).astype(np.float32).astype(dtype).astype(np.float64)
    return np.moveaxis((codes * scale).reshape(v.shape), -1, axis)


WIDE = False


def mx_kscale(k):
    if not WIDE:
        return np.ones(k)
    levels = np.array([30, -30])
    if k % 512:
        return np.exp2(np.random.permutation(np.resize(levels, k // 32))).repeat(32)
    a = np.empty((k // 512, 16))
    for p in range(k // 512):
        a[p, :8] = np.random.permutation(np.resize(levels, 8))
        for g in range(8):
            far = levels[np.abs(levels - a[p, g]) >= 10]
            a[p, g + 8] = far[np.random.randint(len(far))]
    return np.exp2(a.ravel()).repeat(32)


def f64(x):
    return np.asarray(x).astype(np.float64)


def striped(idx):
    return np.tile(np.asarray(idx).reshape(-1, 16).T, (8, 1)).astype(np.uint16)


def unstriped(offs):
    return offs[:16].T.reshape(-1).astype(np.int64)


E2M1 = np.array([0.0, 0.5, 1.0, 1.5, 2.0, 3.0, 4.0, 6.0, -0.0, -0.5, -1.0, -1.5, -2.0, -3.0, -4.0, -6.0])


def pack_weight(w, fmt):
    k, n = w.shape
    w = f64(np.asarray(w, np.float32).astype(ml_dtypes.bfloat16)).reshape(k // 32, 32, n)
    amax = np.abs(w).max(1)
    if fmt in ("e4m3", "e5m2"):
        byte = np.frexp(amax)[1] - 1 + 127 - (7 if fmt == "e4m3" else 14)
    else:
        mant, ex = np.frexp(amax / 6.0)
        byte = np.where(mant > 0.5, ex, ex - 1) + 127
    byte = np.clip(np.where(amax > 0, byte, 1), 1, 254)
    scaled = (w * np.exp2(127.0 - byte)[:, None, :]).reshape(k, n).astype(np.float32)
    by_word = np.ascontiguousarray(scaled.reshape(k // 512, 128, 4, n).transpose(0, 1, 3, 2))
    if fmt in ("e4m3", "e5m2"):
        words = by_word.astype(ml_dtypes.float8_e4m3fn if fmt == "e4m3" else ml_dtypes.float8_e5m2).view(np.uint8)
    else:
        c = by_word.astype(ml_dtypes.float4_e2m1fn).view(np.uint8) & 0xF
        words = (c[..., 0::2] | (c[..., 1::2] << 4)).reshape(k // 512, 128, 2 * n)
    return np.ascontiguousarray(words), np.ascontiguousarray(byte.astype(np.uint8).reshape(k // 512, 16, n))


def unpack_weight(words, scales, fmt):
    g, _, n = scales.shape
    words = np.ascontiguousarray(words).reshape(g, 128, n, -1)
    if fmt in ("e4m3", "e5m2"):
        vals = words.view(ml_dtypes.float8_e4m3fn if fmt == "e4m3" else ml_dtypes.float8_e5m2).astype(np.float64)
    else:
        nib = np.empty((g, 128, n, 4), np.uint8)
        nib[..., 0::2] = words & 0xF
        nib[..., 1::2] = words >> 4
        vals = E2M1[nib]
    vals = vals * np.repeat(np.exp2(scales.astype(np.float64) - 127.0), 8, axis=1)[..., None]
    return vals.transpose(0, 1, 3, 2).reshape(g * 512, n)


def e4m3fn_bytes(y):
    return np.clip(np.asarray(y, np.float64), -448.0, 448.0).astype(np.float32).astype(ml_dtypes.float8_e4m3fn).view(np.uint8)


def e4m3fn_values(b):
    return np.asarray(b, np.uint8).view(ml_dtypes.float8_e4m3fn).astype(np.float64)


K, T, J, R, F, Z, D, N, E = 512, 1024, 256, 512, 512, 1024, 2048, 256, 512


def setup_inputs():
    n = np.random.standard_normal
    idx = np.random.permutation(T)[:J]
    idx2 = np.random.permutation(Z)[:J]
    idx3 = np.random.permutation(E)[:J]
    idx4 = np.random.permutation(D)[:E]
    fk = mx_kscale(K)
    ff = mx_kscale(F)
    fr = mx_kscale(R)
    xtp = pack_weight(n((K, T)) / fk[:, None], "e4m3")
    xop = pack_weight(n((F, Z)) / ff[:, None], "e2m1")
    wp = pack_weight(n((K, R)) * 1 / np.sqrt(K) * fk[:, None] * fr, "e2m1")
    w0p = pack_weight(n((F, R)) * 1 / np.sqrt(F) * ff[:, None] * fr, "e5m2")
    wbp = pack_weight(n((R, N)) * 1 / np.sqrt(R) / fr[:, None], "e5m2")
    return {
        "xt_words": xtp[0],
        "xt_scales": xtp[1],
        "xo_words": xop[0],
        "xo_scales": xop[1],
        "w_words": wp[0],
        "w_scales": wp[1],
        "w0_words": w0p[0],
        "w0_scales": w0p[1],
        "wb_words": wbp[0],
        "wb_scales": wbp[1],
        "so": (np.random.uniform(0.5, 1.6, (N, 1))).astype(np.float32),
        "ca": e4m3fn_bytes(60.0 * n((N, D))),
        "sm": (np.random.uniform(0.004, 0.012, (N, 1))).astype(np.float32),
        "offs": striped(idx),
        "offs2": striped(idx2),
        "offs3": striped(idx3),
        "offs4": striped(idx4),
    }


def reference(xt_words, xt_scales, xo_words, xo_scales, w_words, w_scales, w0_words, w0_scales, wb_words, wb_scales, so, ca, sm, offs, offs2, offs3, offs4):
    idx = unstriped(offs)
    idx2 = unstriped(offs2)
    idx3 = unstriped(offs3)
    idx4 = unstriped(offs4)
    xtu = unpack_weight(xt_words, xt_scales, "e4m3")
    xou = unpack_weight(xo_words, xo_scales, "e2m1")
    wu = unpack_weight(w_words, w_scales, "e2m1")
    w0u = unpack_weight(w0_words, w0_scales, "e5m2")
    wbu = unpack_weight(wb_words, wb_scales, "e5m2")
    xtidxg = xtu[:, idx]
    xoidx2g = xou[:, idx2]
    a = wu.T @ xtidxg + w0u.T @ xoidx2g
    hid = np.maximum(a, 0.0)
    hidq = mxq(hid, 0, "e4m3")
    p = wbu.T @ hidq
    pe = np.zeros((N, E))
    pe[:, idx3] = p * f64(so)
    g1 = e4m3fn_values(ca)[:, idx4] * f64(sm)
    y = np.abs(pe - g1)
    return y

@@ -1,0 +1,209 @@
+from contextlib import ExitStack
+
+import concourse.mybir as mybir
+
+F32 = mybir.dt.float32
+BF16 = mybir.dt.bfloat16
+I32 = mybir.dt.int32
+U32 = mybir.dt.uint32
+U16 = mybir.dt.uint16
+U8 = mybir.dt.uint8
+E4M3 = mybir.dt.float8_e4m3fn
+E4M3X4 = mybir.dt.float8_e4m3fn_x4
+E5M2X4 = mybir.dt.float8_e5m2_x4
+E2M1X4 = mybir.dt.float4_e2m1fn_x4
+ACT = mybir.ActivationFunctionType
+ALU = mybir.AluOpType
+
+P = 128
+T, J, R, Z, D, N, E = 1024, 256, 512, 1024, 2048, 256, 512
+H = 128
+
+FLOPS = 2 * 512 * R * J * 2 + 2 * R * N * J
+
+
+def tile_list_maskedpage_kernel(
+    tc, xt_words, xt_scales, xo_words, xo_scales, w_words, w_scales, w0_words, w0_scales,
+    wb_words, wb_scales, so, ca, sm, offs, offs2, offs3, offs4, out,
+):
+    nc = tc.nc
+    with ExitStack() as ctx:
+        sb = ctx.enter_context(tc.tile_pool(name="sb", bufs=1))
+        ps = ctx.enter_context(tc.psum_pool(name="ps", bufs=1))
+
+        def t(name, shape, dt):
+            return sb.tile(shape, dt, name=name, align_bytes=64)
+
+        l1 = t("l1", [P, J // 16], U16)
+        l2 = t("l2", [P, J // 16], U16)
+        l3 = t("l3", [P, J // 16], U16)
+        l4 = t("l4", [P, E // 16], U16)
+        xtw = t("xtw", [P, T], U32)
+        xts = t("xts", [P, T], U8)
+        xow = t("xow", [P, Z], U16)
+        xos = t("xos", [P, Z], U8)
+        ww = t("ww", [P, R], U16)
+        ws = t("ws", [P, R], U8)
+        w0w = t("w0w", [P, R], U32)
+        w0s = t("w0s", [P, R], U8)
+        wbw = t("wbw", [P, N], U32)
+        wbs = t("wbs", [P, N], U8)
+        wwp = t("wwp", [P, R], U16)
+        wsp = t("wsp", [P, R], U8)
+        w0wp = t("w0wp", [P, R], U32)
+        w0sp = t("w0sp", [P, R], U8)
+        sot = t("sot", [P, 2], F32)
+        smt = t("smt", [P, 2], F32)
+        cat = [t("ca%d" % h, [P, D], U8) for h in range(2)]
+        cag = [t("cag%d" % h, [P, E], U8) for h in range(2)]
+        g1 = [t("g1%d" % h, [P, E], F32) for h in range(2)]
+        pe = [t("pe%d" % h, [P, E], F32) for h in range(2)]
+        df = [t("df%d" % h, [P, E], F32) for h in range(2)]
+        res = [t("res%d" % h, [P, E], F32) for h in range(2)]
+        gxtw = t("gxtw", [P, J], U32)
+        gxts = t("gxts", [P, J], U8)
+        gxow = t("gxow", [P, J], U16)
+        gxos = t("gxos", [P, J], U8)
+        hb = [t("hb%d" % c, [P, H, 4], BF16) for c in range(2)]
+        hq = [t("hq%d" % c, [P, H], U32) for c in range(2)]
+        hs = [t("hs%d" % c, [P, H], U8) for c in range(2)]
+        pt = [t("pt%d" % c, [P, 2, H], F32) for c in range(2)]
+        acc = [ps.tile([P, 4, H], F32, name="acc%d" % c) for c in range(2)]
+        pacc = [ps.tile([P, 2, H], F32, name="pacc%d" % c) for c in range(2)]
+
+        def words(eng, tile, src):
+            eng.dma_start(out=tile[:].bitcast(I32), in_=src.bitcast(I32))
+
+        def scales(eng, tile, src, qs=(0, 1, 2, 3)):
+            for q in qs:
+                eng.dma_start(out=tile[32 * q : 32 * q + 4, :].bitcast(I32), in_=src[0, 4 * q : 4 * q + 4, :].bitcast(I32))
+
+        def col(eng, tile, src):
+            with nc.allow_non_contiguous_dma(reason="one value a partition"):
+                eng.dma_start(out=tile[:], in_=src.rearrange("(h p) o -> p (h o)", p=P))
+
+        def deal(eng_copy, dst, src):
+            eng_copy(out=dst[:].rearrange("p (t m) -> p m t", t=4), in_=src[:].rearrange("p (m t) -> p m t", t=4))
+
+        def gather(dst, win, lst, a, b):
+            nc.vector.tensor_copy(out=dst[:, a:b], in_=win[:].indirect(lst[:, a // 16 : b // 16]))
+
+        def mm1(c, first):
+            cs = slice(c * H, (c + 1) * H)
+            for k in range(4):
+                ms = slice(k * P, (k + 1) * P)
+                if first:
+                    nc.tensor.matmul_mx(out=acc[c][:, k, :], lhsT=wwp[:, ms].bitcast(E2M1X4), lhsT_scale=wsp[:, ms],
+                                        rhs=gxtw[:, cs].bitcast(E4M3X4), rhs_scale=gxts[:, cs], start=(k == 0), stop=False)
+                else:
+                    nc.tensor.matmul_mx(out=acc[c][:, k, :], lhsT=w0wp[:, ms].bitcast(E5M2X4), lhsT_scale=w0sp[:, ms],
+                                        rhs=gxow[:, cs].bitcast(E2M1X4), rhs_scale=gxos[:, cs], start=False, stop=(k == 3))
+
+        def relu_s(c):
+            nc.scalar.activation(out=hb[c][:], in_=acc[c][:].rearrange("p t j -> p j t"), func=ACT.Relu)
+
+        def relu_v(c):
+            nc.vector.tensor_scalar(out=hb[c][:], in0=acc[c][:].rearrange("p t j -> p j t"), scalar1=0.0, scalar2=None, op0=ALU.max)
+
+        def quant(c):
+            nc.vector.quantize_mx(out=hq[c][:].bitcast(E4M3X4), scales=hs[c][:], in_=hb[c][:].rearrange("p j t -> p (j t)"))
+
+        def mm2(c):
+            for h in range(2):
+                ms = slice(h * P, (h + 1) * P)
+                nc.tensor.matmul_mx(out=pacc[c][:, h, :], lhsT=wbw[:, ms].bitcast(E5M2X4), lhsT_scale=wbs[:, ms],
+                                    rhs=hq[c][:].bitcast(E4M3X4), rhs_scale=hs[c][:], start=True, stop=True)
+
+        def put(c, h):
+            nc.scalar.activation(out=pe[h][:].indirect(l3[:, c * 8 : c * 8 + 8]), in_=pt[c][:, h, :], func=ACT.Copy, scale=sot[:, h : h + 1])
+
+        def step(h):
+            nc.scalar.activation(out=g1[h][:], in_=cag[h][:].bitcast(E4M3), func=ACT.Copy, scale=smt[:, h : h + 1])
+
+        def step_v(h):
+            nc.vector.tensor_scalar(out=g1[h][:], in0=cag[h][:].bitcast(E4M3), scalar1=smt[:, h : h + 1], scalar2=None, op0=ALU.mult)
+
+        def sub(h, a, b):
+            nc.vector.tensor_tensor(out=df[h][:, a:b], in0=pe[h][:, a:b], in1=g1[h][:, a:b], op=ALU.subtract)
+
+        def abs_v(h, a, b):
+            nc.vector.scalar_tensor_tensor(out=res[h][:, a:b], in0=df[h][:, a:b], scalar=-1.0, in1=df[h][:, a:b], op0=ALU.mult, op1=ALU.max)
+
+        def abs_s(h, a, b):
+            nc.scalar.activation(out=res[h][:, a:b], in_=df[h][:, a:b], func=ACT.Abs)
+
+        def store(h, a, b, eng=nc.sync):
+            eng.dma_start(out=out[h * P : (h + 1) * P, a:b], in_=res[h][:, a:b])
+
+        xt_src = xt_words[0].rearrange("p n t -> p (n t)")
+        w0_src = w0_words[0].rearrange("p n t -> p (n t)")
+        wb_src = wb_words[0].rearrange("p n t -> p (n t)")
+
+        nc.vector.memset(xts[:].bitcast(I32), 0)
+        nc.vector.memset(ws[:].bitcast(I32), 0)
+        nc.vector.memset(w0s[:].bitcast(I32), 0)
+        nc.vector.memset(xos[:].bitcast(I32), 0)
+        nc.vector.memset(wbs[:].bitcast(I32), 0)
+        nc.vector.memset(pe[0][:], 0.0)
+        nc.vector.memset(pe[1][:], 0.0)
+        nc.sync.dma_start(out=l4[:], in_=offs4)
+        nc.sync.dma_start(out=cat[0][:], in_=ca[0:P, :])
+        nc.sync.dma_start(out=l1[:], in_=offs)
+        words(nc.sync, xtw, xt_src)
+        scales(nc.sync, xts, xt_scales)
+        scales(nc.sync, ws, w_scales)
+        words(nc.sync, ww, w_words[0])
+        nc.sync.dma_start(out=l2[:], in_=offs2)
+        words(nc.sync, xow, xo_words[0])
+        words(nc.sync, w0w, w0_src)
+        scales(nc.sync, w0s, w0_scales)
+        scales(nc.sync, xos, xo_scales)
+        words(nc.sync, wbw, wb_src)
+        nc.sync.dma_start(out=l3[:], in_=offs3)
+        nc.sync.dma_start(out=cat[1][:], in_=ca[P : 2 * P, :])
+        col(nc.gpsimd, smt, sm)
+        scales(nc.gpsimd, wbs, wb_scales)
+        col(nc.gpsimd, sot, so)
+
+        gather(cag[0], cat[0], l4, 0, E)
+        gather(gxtw, xtw, l1, 0, H)
+        gather(gxts, xts, l1, 0, H)
+        step(0)
+        deal(nc.scalar.copy, wwp, ww)
+        deal(nc.vector.tensor_copy, wsp, ws)
+        mm1(0, True)
+        gather(gxow, xow, l2, 0, H)
+        deal(nc.scalar.copy, w0wp, w0w)
+        deal(nc.vector.tensor_copy, w0sp, w0s)
+        gather(gxos, xos, l2, 0, H)
+        mm1(0, False)
+        relu_s(0)
+        gather(gxtw, xtw, l1, H, J)
+        gather(gxts, xts, l1, H, J)
+        mm1(1, True)
+        gather(gxow, xow, l2, H, J)
+        gather(gxos, xos, l2, H, J)
+        mm1(1, False)
+        quant(0)
+        mm2(0)
+        nc.scalar.copy(out=pt[0][:], in_=pacc[0][:])
+        put(0, 0)
+        put(0, 1)
+        relu_v(1)
+        quant(1)
+        mm2(1)
+        nc.vector.tensor_copy(out=pt[1][:], in_=pacc[1][:])
+        put(1, 0)
+        put(1, 1)
+        gather(cag[1], cat[1], l4, 0, 256)
+        gather(cag[1], cat[1], l4, 256, E)
+        step_v(1)
+        sub(0, 0, E)
+        abs_s(0, 0, E)
+        store(0, 0, E)
+        sub(1, 0, 256)
+        sub(1, 256, E)
+        abs_s(1, 0, 256)
+        store(1, 0, 256)
+        abs_v(1, 256, E)
+        store(1, 256, E)

@@ -139,71 +139,123 @@ def tile_list_maskedpage_kernel(
         w0_src = w0_words[0].rearrange("p n t -> p (n t)")
         wb_src = wb_words[0].rearrange("p n t -> p (n t)")
 
-        nc.vector.memset(xts[:].bitcast(I32), 0)
-        nc.vector.memset(ws[:].bitcast(I32), 0)
-        nc.vector.memset(w0s[:].bitcast(I32), 0)
+        ws2 = t("ws2", [P, 2 * R], U8)
+        w0s2 = t("w0s2", [P, 2 * R], U8)
+        wbs2 = t("wbs2", [P, 2 * N], U8)
+
+        def scales2(eng, tile, src):
+            rows = src[0].bitcast(I32).rearrange("(a b r) n -> b r a n", a=2, b=2)
+            for b in range(2):
+                eng.dma_start(out=tile[32 * b : 32 * b + 4, :].bitcast(I32).rearrange("p (a n) -> p a n", a=2), in_=rows[b])
+
+        def lift(tile, n):
+            nc.vector.tensor_copy(out=tile[64:128, 0:n].bitcast(I32), in_=tile[0:64, n : 2 * n].bitcast(I32))
+
+        def deal2(dst, src):
+            nc.vector.tensor_copy(out=dst[:].rearrange("p (t m) -> p m t", t=4), in_=src[:, 0:R].rearrange("p (m t) -> p m t", t=4))
+
+        def mm2b(c):
+            for h in range(2):
+                ms = slice(h * P, (h + 1) * P)
+                nc.tensor.matmul_mx(out=pacc[c][:, h, :], lhsT=wbw[:, ms].bitcast(E5M2X4), lhsT_scale=wbs[:, ms],
+                                    rhs=hq[c][:].bitcast(E4M3X4), rhs_scale=hs[c][:], start=True, stop=True)
+
+        xts2 = t("xts2", [64, 2 * T], U8)
+        xos2 = t("xos2", [64, 2 * Z], U8)
+
+        def spread(dst, src, n):
+            nc.vector.tensor_copy(out=dst[0:64, :].bitcast(I32), in_=src[0:64, 0:n].bitcast(I32))
+            nc.vector.tensor_copy(out=dst[64:128, :].bitcast(I32), in_=src[0:64, n : 2 * n].bitcast(I32))
+
+        def deal_g(dst, src):
+            nc.gpsimd.tensor_copy(out=dst[:].rearrange("p (t m) -> p t m", t=4), in_=src[:, 0:R].rearrange("p (m t) -> p t m", t=4))
+
+        def widen(h):
+            nc.gpsimd.tensor_copy(out=g1[h][:], in_=cag[h][:].bitcast(E4M3))
+
+        def sub2(h, a, b):
+            nc.vector.scalar_tensor_tensor(out=df[h][:, a:b], in0=g1[h][:, a:b], scalar=smt[:, h : h + 1], in1=pe[h][:, a:b], op0=ALU.mult, op1=ALU.subtract)
+
+        pr = [t("pr%d" % h, [P, J], F32) for h in range(2)]
+        pa0 = [ps.tile([P, H], F32, name="pa0%d" % c) for c in range(2)]
+        pa1 = ps.tile([P, J], F32, name="pa1")
+
+        def mm2h(c, h):
+            ms = slice(h * P, (h + 1) * P)
+            dst = pa0[c][:] if h == 1 else pa1[:, c * H : (c + 1) * H]
+            nc.tensor.matmul_mx(out=dst, lhsT=wbw[:, ms].bitcast(E5M2X4), lhsT_scale=wbs[:, ms],
+                                rhs=hq[c][:].bitcast(E4M3X4), rhs_scale=hs[c][:], start=True, stop=True)
+
+        def put2(h, a, b):
+            nc.scalar.activation(out=pe[h][:].indirect(l3[:, a // 16 : b // 16]), in_=pr[h][:, a:b], func=ACT.Copy, scale=sot[:, h : h + 1])
+
+        nc.vector.memset(ws2[0:64, :].bitcast(I32), 0)
+        nc.vector.memset(w0s2[0:64, :].bitcast(I32), 0)
+        nc.vector.memset(xts2[:].bitcast(I32), 0)
         nc.vector.memset(xos[:].bitcast(I32), 0)
         nc.vector.memset(wbs[:].bitcast(I32), 0)
         nc.vector.memset(pe[0][:], 0.0)
         nc.vector.memset(pe[1][:], 0.0)
-        nc.sync.dma_start(out=l4[:], in_=offs4)
-        nc.sync.dma_start(out=cat[0][:], in_=ca[0:P, :])
+        words(nc.gpsimd, ww, w_words[0])
         nc.sync.dma_start(out=l1[:], in_=offs)
+        scales2(nc.sync, ws2, w_scales)
+        scales2(nc.sync, w0s2, w0_scales)
+        scales2(nc.sync, xts2, xt_scales)
         words(nc.sync, xtw, xt_src)
-        scales(nc.sync, xts, xt_scales)
-        scales(nc.sync, ws, w_scales)
-        words(nc.sync, ww, w_words[0])
-        nc.sync.dma_start(out=l2[:], in_=offs2)
-        words(nc.sync, xow, xo_words[0])
         words(nc.sync, w0w, w0_src)
-        scales(nc.sync, w0s, w0_scales)
+        words(nc.sync, xow, xo_words[0])
+        nc.sync.dma_start(out=l2[:], in_=offs2)
         scales(nc.sync, xos, xo_scales)
+        nc.sync.dma_start(out=cat[0][:], in_=ca[0:P, :])
+        nc.sync.dma_start(out=l4[:], in_=offs4)
+        scales(nc.sync, wbs, wb_scales)
         words(nc.sync, wbw, wb_src)
         nc.sync.dma_start(out=l3[:], in_=offs3)
+        col(nc.sync, sot, so)
         nc.sync.dma_start(out=cat[1][:], in_=ca[P : 2 * P, :])
-        col(nc.gpsimd, smt, sm)
-        scales(nc.gpsimd, wbs, wb_scales)
-        col(nc.gpsimd, sot, so)
+        col(nc.sync, smt, sm)
 
-        gather(cag[0], cat[0], l4, 0, E)
-        gather(gxtw, xtw, l1, 0, H)
-        gather(gxts, xts, l1, 0, H)
-        step(0)
+        lift(ws2, R)
+        deal2(wsp, ws2)
+        lift(w0s2, R)
+        deal2(w0sp, w0s2)
+        spread(xts, xts2, T)
         deal(nc.scalar.copy, wwp, ww)
-        deal(nc.vector.tensor_copy, wsp, ws)
-        mm1(0, True)
-        gather(gxow, xow, l2, 0, H)
         deal(nc.scalar.copy, w0wp, w0w)
-        deal(nc.vector.tensor_copy, w0sp, w0s)
+        gather(gxts, xts, l1, 0, J)
+        gather(gxtw, xtw, l1, 0, J)
+        mm1(0, True)
+        mm1(1, True)
+        gather(gxow, xow, l2, 0, J)
         gather(gxos, xos, l2, 0, H)
         mm1(0, False)
         relu_s(0)
-        gather(gxtw, xtw, l1, H, J)
-        gather(gxts, xts, l1, H, J)
-        mm1(1, True)
-        gather(gxow, xow, l2, H, J)
         gather(gxos, xos, l2, H, J)
         mm1(1, False)
+        relu_s(1)
+        gather(cag[0], cat[0], l4, 0, E)
         quant(0)
-        mm2(0)
-        nc.scalar.copy(out=pt[0][:], in_=pacc[0][:])
-        put(0, 0)
-        put(0, 1)
-        relu_v(1)
+        mm2h(0, 1)
         quant(1)
-        mm2(1)
-        nc.vector.tensor_copy(out=pt[1][:], in_=pacc[1][:])
-        put(1, 0)
-        put(1, 1)
-        gather(cag[1], cat[1], l4, 0, 256)
-        gather(cag[1], cat[1], l4, 256, E)
+        nc.vector.tensor_copy(out=pr[1][:, 0:H], in_=pa0[0][:])
+        put2(1, 0, H)
+        mm2h(0, 0)
+        mm2h(1, 0)
+        mm2h(1, 1)
+        nc.vector.tensor_copy(out=pr[0][:], in_=pa1[:])
+        put2(0, 0, J)
+        nc.vector.tensor_copy(out=pr[1][:, H:J], in_=pa0[1][:])
+        put2(1, H, J)
+
+        gather(cag[1], cat[1], l4, 0, E)
+        step_v(0)
         step_v(1)
         sub(0, 0, E)
         abs_s(0, 0, E)
         store(0, 0, E)
         sub(1, 0, 256)
         sub(1, 256, E)
-        abs_s(1, 0, 256)
+        abs_v(1, 0, 256)
         store(1, 0, 256)
-        abs_v(1, 256, E)
+        abs_s(1, 256, E)
         store(1, 256, E)

@@ -189,6 +189,13 @@ def tile_list_maskedpage_kernel(
         def put2(h, a, b):
             nc.scalar.activation(out=pe[h][:].indirect(l3[:, a // 16 : b // 16]), in_=pr[h][:, a:b], func=ACT.Copy, scale=sot[:, h : h + 1])
 
+        def deal_r(eng_copy, dst, src):
+            eng_copy(out=dst[:].rearrange("p (t m) -> p t m", t=4), in_=src[:, 0:R].rearrange("p (m t) -> p t m", t=4))
+
+        def half(eng, tile, src, b):
+            rows = src[0].bitcast(I32).rearrange("(a b r) n -> b r a n", a=2, b=2)
+            eng.dma_start(out=tile[32 * b : 32 * b + 4, :].bitcast(I32).rearrange("p (a n) -> p a n", a=2), in_=rows[b])
+
         nc.vector.memset(ws2[0:64, :].bitcast(I32), 0)
         nc.vector.memset(w0s2[0:64, :].bitcast(I32), 0)
         nc.vector.memset(xts2[:].bitcast(I32), 0)
@@ -196,31 +203,32 @@ def tile_list_maskedpage_kernel(
         nc.vector.memset(wbs[:].bitcast(I32), 0)
         nc.vector.memset(pe[0][:], 0.0)
         nc.vector.memset(pe[1][:], 0.0)
-        words(nc.gpsimd, ww, w_words[0])
         nc.sync.dma_start(out=l1[:], in_=offs)
         scales2(nc.sync, ws2, w_scales)
-        scales2(nc.sync, w0s2, w0_scales)
-        scales2(nc.sync, xts2, xt_scales)
+        scales2(nc.scalar, w0s2, w0_scales)
+        half(nc.sync, xts2, xt_scales, 0)
+        half(nc.scalar, xts2, xt_scales, 1)
         words(nc.sync, xtw, xt_src)
-        words(nc.sync, w0w, w0_src)
-        words(nc.sync, xow, xo_words[0])
         nc.sync.dma_start(out=l2[:], in_=offs2)
+        words(nc.sync, ww, w_words[0])
+        words(nc.sync, xow, xo_words[0])
+        words(nc.sync, w0w, w0_src)
         scales(nc.sync, xos, xo_scales)
         nc.sync.dma_start(out=cat[0][:], in_=ca[0:P, :])
         nc.sync.dma_start(out=l4[:], in_=offs4)
         scales(nc.sync, wbs, wb_scales)
         words(nc.sync, wbw, wb_src)
-        nc.sync.dma_start(out=l3[:], in_=offs3)
         col(nc.sync, sot, so)
-        nc.sync.dma_start(out=cat[1][:], in_=ca[P : 2 * P, :])
         col(nc.sync, smt, sm)
+        nc.sync.dma_start(out=cat[1][:], in_=ca[P : 2 * P, :])
+        nc.sync.dma_start(out=l3[:], in_=offs3)
 
         lift(ws2, R)
-        deal2(wsp, ws2)
         lift(w0s2, R)
-        deal2(w0sp, w0s2)
+        deal_r(nc.vector.tensor_copy, wsp, ws2)
+        deal_r(nc.vector.tensor_copy, w0sp, w0s2)
         spread(xts, xts2, T)
-        deal(nc.scalar.copy, wwp, ww)
+        deal_r(nc.scalar.copy, wwp, ww)
         deal(nc.scalar.copy, w0wp, w0w)
         gather(gxts, xts, l1, 0, J)
         gather(gxtw, xtw, l1, 0, J)
@@ -234,6 +242,7 @@ def tile_list_maskedpage_kernel(
         mm1(1, False)
         relu_s(1)
         gather(cag[0], cat[0], l4, 0, E)
+        step(0)
         quant(0)
         mm2h(0, 1)
         quant(1)
@@ -248,7 +257,6 @@ def tile_list_maskedpage_kernel(
         put2(1, H, J)
 
         gather(cag[1], cat[1], l4, 0, E)
-        step_v(0)
         step_v(1)
         sub(0, 0, E)
         abs_s(0, 0, E)

@@ -196,37 +196,62 @@ def tile_list_maskedpage_kernel(
             rows = src[0].bitcast(I32).rearrange("(a b r) n -> b r a n", a=2, b=2)
             eng.dma_start(out=tile[32 * b : 32 * b + 4, :].bitcast(I32).rearrange("p (a n) -> p a n", a=2), in_=rows[b])
 
-        nc.vector.memset(ws2[0:64, :].bitcast(I32), 0)
-        nc.vector.memset(w0s2[0:64, :].bitcast(I32), 0)
+        def mm_o(c):
+            cs = slice(c * H, (c + 1) * H)
+            for k in range(4):
+                ms = slice(k * P, (k + 1) * P)
+                nc.tensor.matmul_mx(out=acc[c][:, k, :], lhsT=w0wp[:, ms].bitcast(E5M2X4), lhsT_scale=w0sp[:, ms],
+                                    rhs=gxow[:, cs].bitcast(E2M1X4), rhs_scale=gxos[:, cs], start=(k == 0), stop=False)
+
+        def mm_t(c):
+            cs = slice(c * H, (c + 1) * H)
+            for k in range(4):
+                ms = slice(k * P, (k + 1) * P)
+                nc.tensor.matmul_mx(out=acc[c][:, k, :], lhsT=wwp[:, ms].bitcast(E2M1X4), lhsT_scale=wsp[:, ms],
+                                    rhs=gxtw[:, cs].bitcast(E4M3X4), rhs_scale=gxts[:, cs], start=False, stop=(k == 3))
+
+        def scales_up(eng, tile, src):
+            rows = src[0].bitcast(I32).rearrange("(a b r) n -> b r a n", a=2, b=2)
+            for b in range(2):
+                eng.dma_start(out=tile[64 + 32 * b : 64 + 32 * b + 4, :].bitcast(I32).rearrange("p (a n) -> p a n", a=2), in_=rows[b])
+
+        def lower(tile):
+            nc.vector.tensor_copy(out=tile[0:64, R : 2 * R].bitcast(I32), in_=tile[64:128, 0:R].bitcast(I32))
+
+        def deal_u(dst, src):
+            nc.vector.tensor_copy(out=dst[:].rearrange("p (t m) -> p t m", t=4), in_=src[:, R : 2 * R].rearrange("p (m t) -> p t m", t=4))
+
+        nc.vector.memset(ws2[64:128, :].bitcast(I32), 0)
+        nc.vector.memset(w0s2[64:128, :].bitcast(I32), 0)
         nc.vector.memset(xts2[:].bitcast(I32), 0)
         nc.vector.memset(xos[:].bitcast(I32), 0)
         nc.vector.memset(wbs[:].bitcast(I32), 0)
         nc.vector.memset(pe[0][:], 0.0)
         nc.vector.memset(pe[1][:], 0.0)
+        words(nc.gpsimd, ww, w_words[0])
+        words(nc.gpsimd, wbw, wb_src)
+        col(nc.gpsimd, sot, so)
         nc.sync.dma_start(out=l1[:], in_=offs)
-        scales2(nc.sync, ws2, w_scales)
-        scales2(nc.scalar, w0s2, w0_scales)
+        scales_up(nc.sync, ws2, w_scales)
+        scales_up(nc.scalar, w0s2, w0_scales)
         half(nc.sync, xts2, xt_scales, 0)
         half(nc.scalar, xts2, xt_scales, 1)
         words(nc.sync, xtw, xt_src)
-        nc.sync.dma_start(out=l2[:], in_=offs2)
-        words(nc.sync, ww, w_words[0])
-        words(nc.sync, xow, xo_words[0])
         words(nc.sync, w0w, w0_src)
+        words(nc.sync, xow, xo_words[0])
+        nc.sync.dma_start(out=l2[:], in_=offs2)
         scales(nc.sync, xos, xo_scales)
         nc.sync.dma_start(out=cat[0][:], in_=ca[0:P, :])
         nc.sync.dma_start(out=l4[:], in_=offs4)
         scales(nc.sync, wbs, wb_scales)
-        words(nc.sync, wbw, wb_src)
-        col(nc.sync, sot, so)
-        col(nc.sync, smt, sm)
-        nc.sync.dma_start(out=cat[1][:], in_=ca[P : 2 * P, :])
         nc.sync.dma_start(out=l3[:], in_=offs3)
+        nc.sync.dma_start(out=cat[1][:], in_=ca[P : 2 * P, :])
+        col(nc.sync, smt, sm)
 
-        lift(ws2, R)
-        lift(w0s2, R)
-        deal_r(nc.vector.tensor_copy, wsp, ws2)
-        deal_r(nc.vector.tensor_copy, w0sp, w0s2)
+        lower(ws2)
+        lower(w0s2)
+        deal_u(wsp, ws2)
+        deal_u(w0sp, w0s2)
         spread(xts, xts2, T)
         deal_r(nc.scalar.copy, wwp, ww)
         deal(nc.scalar.copy, w0wp, w0w)
@@ -242,7 +267,6 @@ def tile_list_maskedpage_kernel(
         mm1(1, False)
         relu_s(1)
         gather(cag[0], cat[0], l4, 0, E)
-        step(0)
         quant(0)
         mm2h(0, 1)
         quant(1)
@@ -257,6 +281,7 @@ def tile_list_maskedpage_kernel(
         put2(1, H, J)
 
         gather(cag[1], cat[1], l4, 0, E)
+        step_v(0)
         step_v(1)
         sub(0, 0, E)
         abs_s(0, 0, E)

from contextlib import ExitStack

import concourse.mybir as mybir

F32 = mybir.dt.float32
BF16 = mybir.dt.bfloat16
I32 = mybir.dt.int32
U32 = mybir.dt.uint32
U16 = mybir.dt.uint16
U8 = mybir.dt.uint8
E4M3 = mybir.dt.float8_e4m3fn
E4M3X4 = mybir.dt.float8_e4m3fn_x4
E5M2X4 = mybir.dt.float8_e5m2_x4
E2M1X4 = mybir.dt.float4_e2m1fn_x4
ACT = mybir.ActivationFunctionType
ALU = mybir.AluOpType

P = 128
T, J, R, Z, D, N, E = 1024, 256, 512, 1024, 2048, 256, 512
H = 128

FLOPS = 2 * 512 * R * J * 2 + 2 * R * N * J


def tile_list_maskedpage_kernel(
    tc, xt_words, xt_scales, xo_words, xo_scales, w_words, w_scales, w0_words, w0_scales,
    wb_words, wb_scales, so, ca, sm, offs, offs2, offs3, offs4, out,
):
    nc = tc.nc
    with ExitStack() as ctx:
        sb = ctx.enter_context(tc.tile_pool(name="sb", bufs=1))
        ps = ctx.enter_context(tc.psum_pool(name="ps", bufs=1))

        def t(name, shape, dt):
            return sb.tile(shape, dt, name=name, align_bytes=64)

        l1 = t("l1", [P, J // 16], U16)
        l2 = t("l2", [P, J // 16], U16)
        l3 = t("l3", [P, J // 16], U16)
        l4 = t("l4", [P, E // 16], U16)
        xtw = t("xtw", [P, T], U32)
        xts = t("xts", [P, T], U8)
        xow = t("xow", [P, Z], U16)
        xos = t("xos", [P, Z], U8)
        ww = t("ww", [P, R], U16)
        ws = t("ws", [P, R], U8)
        w0w = t("w0w", [P, R], U32)
        w0s = t("w0s", [P, R], U8)
        wbw = t("wbw", [P, N], U32)
        wbs = t("wbs", [P, N], U8)
        wwp = t("wwp", [P, R], U16)
        wsp = t("wsp", [P, R], U8)
        w0wp = t("w0wp", [P, R], U32)
        w0sp = t("w0sp", [P, R], U8)
        sot = t("sot", [P, 2], F32)
        smt = t("smt", [P, 2], F32)
        cat = [t("ca%d" % h, [P, D], U8) for h in range(2)]
        cag = [t("cag%d" % h, [P, E], U8) for h in range(2)]
        g1 = [t("g1%d" % h, [P, E], F32) for h in range(2)]
        pe = [t("pe%d" % h, [P, E], F32) for h in range(2)]
        df = [t("df%d" % h, [P, E], F32) for h in range(2)]
        res = [t("res%d" % h, [P, E], F32) for h in range(2)]
        gxtw = t("gxtw", [P, J], U32)
        gxts = t("gxts", [P, J], U8)
        gxow = t("gxow", [P, J], U16)
        gxos = t("gxos", [P, J], U8)
        hb = [t("hb%d" % c, [P, H, 4], BF16) for c in range(2)]
        hq = [t("hq%d" % c, [P, H], U32) for c in range(2)]
        hs = [t("hs%d" % c, [P, H], U8) for c in range(2)]
        pt = [t("pt%d" % c, [P, 2, H], F32) for c in range(2)]
        acc = [ps.tile([P, 4, H], F32, name="acc%d" % c) for c in range(2)]
        pacc = [ps.tile([P, 2, H], F32, name="pacc%d" % c) for c in range(2)]

        def words(eng, tile, src):
            eng.dma_start(out=tile[:].bitcast(I32), in_=src.bitcast(I32))

        def scales(eng, tile, src, qs=(0, 1, 2, 3)):
            for q in qs:
                eng.dma_start(out=tile[32 * q : 32 * q + 4, :].bitcast(I32), in_=src[0, 4 * q : 4 * q + 4, :].bitcast(I32))

        def col(eng, tile, src):
            with nc.allow_non_contiguous_dma(reason="one value a partition"):
                eng.dma_start(out=tile[:], in_=src.rearrange("(h p) o -> p (h o)", p=P))

        def deal(eng_copy, dst, src):
            eng_copy(out=dst[:].rearrange("p (t m) -> p m t", t=4), in_=src[:].rearrange("p (m t) -> p m t", t=4))

        def gather(dst, win, lst, a, b):
            nc.vector.tensor_copy(out=dst[:, a:b], in_=win[:].indirect(lst[:, a // 16 : b // 16]))

        def mm1(c, first):
            cs = slice(c * H, (c + 1) * H)
            for k in range(4):
                ms = slice(k * P, (k + 1) * P)
                if first:
                    nc.tensor.matmul_mx(out=acc[c][:, k, :], lhsT=wwp[:, ms].bitcast(E2M1X4), lhsT_scale=wsp[:, ms],
                                        rhs=gxtw[:, cs].bitcast(E4M3X4), rhs_scale=gxts[:, cs], start=(k == 0), stop=False)
                else:
                    nc.tensor.matmul_mx(out=acc[c][:, k, :], lhsT=w0wp[:, ms].bitcast(E5M2X4), lhsT_scale=w0sp[:, ms],
                                        rhs=gxow[:, cs].bitcast(E2M1X4), rhs_scale=gxos[:, cs], start=False, stop=(k == 3))

        def relu_s(c):
            nc.scalar.activation(out=hb[c][:], in_=acc[c][:].rearrange("p t j -> p j t"), func=ACT.Relu)

        def relu_v(c):
            nc.vector.tensor_scalar(out=hb[c][:], in0=acc[c][:].rearrange("p t j -> p j t"), scalar1=0.0, scalar2=None, op0=ALU.max)

        def quant(c):
            nc.vector.quantize_mx(out=hq[c][:].bitcast(E4M3X4), scales=hs[c][:], in_=hb[c][:].rearrange("p j t -> p (j t)"))

        def mm2(c):
            for h in range(2):
                ms = slice(h * P, (h + 1) * P)
                nc.tensor.matmul_mx(out=pacc[c][:, h, :], lhsT=wbw[:, ms].bitcast(E5M2X4), lhsT_scale=wbs[:, ms],
                                    rhs=hq[c][:].bitcast(E4M3X4), rhs_scale=hs[c][:], start=True, stop=True)

        def put(c, h):
            nc.scalar.activation(out=pe[h][:].indirect(l3[:, c * 8 : c * 8 + 8]), in_=pt[c][:, h, :], func=ACT.Copy, scale=sot[:, h : h + 1])

        def step(h):
            nc.scalar.activation(out=g1[h][:], in_=cag[h][:].bitcast(E4M3), func=ACT.Copy, scale=smt[:, h : h + 1])

        def step_v(h):
            nc.vector.tensor_scalar(out=g1[h][:], in0=cag[h][:].bitcast(E4M3), scalar1=smt[:, h : h + 1], scalar2=None, op0=ALU.mult)

        def sub(h, a, b):
            nc.vector.tensor_tensor(out=df[h][:, a:b], in0=pe[h][:, a:b], in1=g1[h][:, a:b], op=ALU.subtract)

        def abs_v(h, a, b):
            nc.vector.scalar_tensor_tensor(out=res[h][:, a:b], in0=df[h][:, a:b], scalar=-1.0, in1=df[h][:, a:b], op0=ALU.mult, op1=ALU.max)

        def abs_s(h, a, b):
            nc.scalar.activation(out=res[h][:, a:b], in_=df[h][:, a:b], func=ACT.Abs)

        def store(h, a, b, eng=nc.sync):
            eng.dma_start(out=out[h * P : (h + 1) * P, a:b], in_=res[h][:, a:b])

        xt_src = xt_words[0].rearrange("p n t -> p (n t)")
        w0_src = w0_words[0].rearrange("p n t -> p (n t)")
        wb_src = wb_words[0].rearrange("p n t -> p (n t)")

        ws2 = t("ws2", [P, 2 * R], U8)
        w0s2 = t("w0s2", [P, 2 * R], U8)
        wbs2 = t("wbs2", [P, 2 * N], U8)

        def scales2(eng, tile, src):
            rows = src[0].bitcast(I32).rearrange("(a b r) n -> b r a n", a=2, b=2)
            for b in range(2):
                eng.dma_start(out=tile[32 * b : 32 * b + 4, :].bitcast(I32).rearrange("p (a n) -> p a n", a=2), in_=rows[b])

        def lift(tile, n):
            nc.vector.tensor_copy(out=tile[64:128, 0:n].bitcast(I32), in_=tile[0:64, n : 2 * n].bitcast(I32))

        def deal2(dst, src):
            nc.vector.tensor_copy(out=dst[:].rearrange("p (t m) -> p m t", t=4), in_=src[:, 0:R].rearrange("p (m t) -> p m t", t=4))

        def mm2b(c):
            for h in range(2):
                ms = slice(h * P, (h + 1) * P)
                nc.tensor.matmul_mx(out=pacc[c][:, h, :], lhsT=wbw[:, ms].bitcast(E5M2X4), lhsT_scale=wbs[:, ms],
                                    rhs=hq[c][:].bitcast(E4M3X4), rhs_scale=hs[c][:], start=True, stop=True)

        xts2 = t("xts2", [64, 2 * T], U8)
        xos2 = t("xos2", [64, 2 * Z], U8)

        def spread(dst, src, n):
            nc.vector.tensor_copy(out=dst[0:64, :].bitcast(I32), in_=src[0:64, 0:n].bitcast(I32))
            nc.vector.tensor_copy(out=dst[64:128, :].bitcast(I32), in_=src[0:64, n : 2 * n].bitcast(I32))

        def deal_g(dst, src):
            nc.gpsimd.tensor_copy(out=dst[:].rearrange("p (t m) -> p t m", t=4), in_=src[:, 0:R].rearrange("p (m t) -> p t m", t=4))

        def widen(h):
            nc.gpsimd.tensor_copy(out=g1[h][:], in_=cag[h][:].bitcast(E4M3))

        def sub2(h, a, b):
            nc.vector.scalar_tensor_tensor(out=df[h][:, a:b], in0=g1[h][:, a:b], scalar=smt[:, h : h + 1], in1=pe[h][:, a:b], op0=ALU.mult, op1=ALU.subtract)

        pr = [t("pr%d" % h, [P, J], F32) for h in range(2)]
        pa0 = [ps.tile([P, H], F32, name="pa0%d" % c) for c in range(2)]
        pa1 = ps.tile([P, J], F32, name="pa1")

        def mm2h(c, h):
            ms = slice(h * P, (h + 1) * P)
            dst = pa0[c][:] if h == 1 else pa1[:, c * H : (c + 1) * H]
            nc.tensor.matmul_mx(out=dst, lhsT=wbw[:, ms].bitcast(E5M2X4), lhsT_scale=wbs[:, ms],
                                rhs=hq[c][:].bitcast(E4M3X4), rhs_scale=hs[c][:], start=True, stop=True)

        def put2(h, a, b):
            nc.scalar.activation(out=pe[h][:].indirect(l3[:, a // 16 : b // 16]), in_=pr[h][:, a:b], func=ACT.Copy, scale=sot[:, h : h + 1])

        def deal_r(eng_copy, dst, src):
            eng_copy(out=dst[:].rearrange("p (t m) -> p t m", t=4), in_=src[:, 0:R].rearrange("p (m t) -> p t m", t=4))

        def half(eng, tile, src, b):
            rows = src[0].bitcast(I32).rearrange("(a b r) n -> b r a n", a=2, b=2)
            eng.dma_start(out=tile[32 * b : 32 * b + 4, :].bitcast(I32).rearrange("p (a n) -> p a n", a=2), in_=rows[b])

        def mm_o(c):
            cs = slice(c * H, (c + 1) * H)
            for k in range(4):
                ms = slice(k * P, (k + 1) * P)
                nc.tensor.matmul_mx(out=acc[c][:, k, :], lhsT=w0wp[:, ms].bitcast(E5M2X4), lhsT_scale=w0sp[:, ms],
                                    rhs=gxow[:, cs].bitcast(E2M1X4), rhs_scale=gxos[:, cs], start=(k == 0), stop=False)

        def mm_t(c):
            cs = slice(c * H, (c + 1) * H)
            for k in range(4):
                ms = slice(k * P, (k + 1) * P)
                nc.tensor.matmul_mx(out=acc[c][:, k, :], lhsT=wwp[:, ms].bitcast(E2M1X4), lhsT_scale=wsp[:, ms],
                                    rhs=gxtw[:, cs].bitcast(E4M3X4), rhs_scale=gxts[:, cs], start=False, stop=(k == 3))

        def scales_up(eng, tile, src):
            rows = src[0].bitcast(I32).rearrange("(a b r) n -> b r a n", a=2, b=2)
            for b in range(2):
                eng.dma_start(out=tile[64 + 32 * b : 64 + 32 * b + 4, :].bitcast(I32).rearrange("p (a n) -> p a n", a=2), in_=rows[b])

        def lower(tile):
            nc.vector.tensor_copy(out=tile[0:64, R : 2 * R].bitcast(I32), in_=tile[64:128, 0:R].bitcast(I32))

        def deal_u(dst, src):
            nc.vector.tensor_copy(out=dst[:].rearrange("p (t m) -> p t m", t=4), in_=src[:, R : 2 * R].rearrange("p (m t) -> p t m", t=4))

        nc.vector.memset(ws2[64:128, :].bitcast(I32), 0)
        nc.vector.memset(w0s2[64:128, :].bitcast(I32), 0)
        nc.vector.memset(xts2[:].bitcast(I32), 0)
        nc.vector.memset(xos[:].bitcast(I32), 0)
        nc.vector.memset(wbs[:].bitcast(I32), 0)
        nc.vector.memset(pe[0][:], 0.0)
        nc.vector.memset(pe[1][:], 0.0)
        words(nc.gpsimd, ww, w_words[0])
        words(nc.gpsimd, wbw, wb_src)
        col(nc.gpsimd, sot, so)
        nc.sync.dma_start(out=l1[:], in_=offs)
        scales_up(nc.sync, ws2, w_scales)
        scales_up(nc.scalar, w0s2, w0_scales)
        half(nc.sync, xts2, xt_scales, 0)
        half(nc.scalar, xts2, xt_scales, 1)
        words(nc.sync, xtw, xt_src)
        words(nc.sync, w0w, w0_src)
        words(nc.sync, xow, xo_words[0])
        nc.sync.dma_start(out=l2[:], in_=offs2)
        scales(nc.sync, xos, xo_scales)
        nc.sync.dma_start(out=cat[0][:], in_=ca[0:P, :])
        nc.sync.dma_start(out=l4[:], in_=offs4)
        scales(nc.sync, wbs, wb_scales)
        nc.sync.dma_start(out=l3[:], in_=offs3)
        nc.sync.dma_start(out=cat[1][:], in_=ca[P : 2 * P, :])
        col(nc.sync, smt, sm)

        lower(ws2)
        lower(w0s2)
        deal_u(wsp, ws2)
        deal_u(w0sp, w0s2)
        spread(xts, xts2, T)
        deal_r(nc.scalar.copy, wwp, ww)
        deal(nc.scalar.copy, w0wp, w0w)
        gather(gxts, xts, l1, 0, J)
        gather(gxtw, xtw, l1, 0, J)
        mm1(0, True)
        mm1(1, True)
        gather(gxow, xow, l2, 0, J)
        gather(gxos, xos, l2, 0, H)
        mm1(0, False)
        relu_s(0)
        gather(gxos, xos, l2, H, J)
        mm1(1, False)
        relu_s(1)
        gather(cag[0], cat[0], l4, 0, E)
        quant(0)
        mm2h(0, 1)
        quant(1)
        nc.vector.tensor_copy(out=pr[1][:, 0:H], in_=pa0[0][:])
        put2(1, 0, H)
        mm2h(0, 0)
        mm2h(1, 0)
        mm2h(1, 1)
        nc.vector.tensor_copy(out=pr[0][:], in_=pa1[:])
        put2(0, 0, J)
        nc.vector.tensor_copy(out=pr[1][:, H:J], in_=pa0[1][:])
        put2(1, H, J)

        gather(cag[1], cat[1], l4, 0, E)
        step_v(0)
        step_v(1)
        sub(0, 0, E)
        abs_s(0, 0, E)
        store(0, 0, E)
        sub(1, 0, 256)
        sub(1, 256, E)
        abs_v(1, 0, 256)
        store(1, 0, 256)
        abs_s(1, 256, E)
        store(1, 256, E)
